import numpy as np
import ml_dtypes


def mxq(x, axis, fmt="e4m3"):
    dtype, down = {"e4m3": (ml_dtypes.float8_e4m3fn, 7), "e5m2": (ml_dtypes.float8_e5m2, 14)}[fmt]
    v = np.moveaxis(np.asarray(x, np.float32).astype(ml_dtypes.bfloat16).astype(np.float64), axis, -1)
    blocks = v.reshape(v.shape[:-1] + (-1, 32))
    amax = np.abs(blocks).max(-1, keepdims=True)
    byte = np.maximum(np.where(amax > 0, np.frexp(amax)[1] - 1 + 127, 0) - down, 1)
    scale = np.exp2(byte - 127.0)
    codes = (blocks / scale).astype(np.float32).astype(dtype).astype(np.float64)
    return np.moveaxis((codes * scale).reshape(v.shape), -1, axis)


WIDE = False


def mx_kscale(k):
    if not WIDE:
        return np.ones(k)
    levels = np.array([10, -10, 5, -5, 0])
    if k % 512:
        return np.exp2(np.random.permutation(np.resize(levels, k // 32))).repeat(32)
    a = np.empty((k // 512, 16))
    for p in range(k // 512):
        a[p, :8] = np.random.permutation(np.resize(levels, 8))
        for g in range(8):
            far = levels[np.abs(levels - a[p, g]) >= 10]
            a[p, g + 8] = far[np.random.randint(len(far))]
    return np.exp2(a.ravel()).repeat(32)


def f64(x):
    return np.asarray(x).astype(np.float64)


def striped(idx):
    return np.tile(idx.reshape(-1, 16).T, (8, 1)).astype(np.uint16)


def unstriped(offs):
    return offs[:16].T.reshape(-1).astype(np.int64)


def relu(v):
    return np.maximum(v, 0.0)


K, T, D, V, H, N = 512, 512, 4, 256, 1024, 256
P = 2 ** 7


def setup_inputs():
    n = np.random.standard_normal
    s = mx_kscale(K)[:, None]
    u = mx_kscale(H)
    return {
        "xT": (n((K, T)) * s).astype(np.float32),
        "w1": (n((K, H)) / np.sqrt(K) / s * u).astype(np.float32),
        "w2": (n((H, N)) / np.sqrt(H) / u[:, None]).astype(np.float32),
        "gate": np.tile(np.random.uniform(0.2, 1.0, (D, 1, V)) / np.sqrt(D), (1, P, 1)).astype(np.float32),
        "pos1": striped(np.random.permutation(T)[:V]),
        "pos2": striped(np.random.permutation(T)[:V]),
        "pos3": striped(np.random.permutation(T)[:V]),
        "pos4": striped(np.random.permutation(T)[:V]),
    }


def reference(xT, w1, w2, gate, pos1, pos2, pos3, pos4):
    h = relu(mxq(f64(w1), 0, "e4m3").T @ mxq(f64(xT), 0, "e4m3"))
    z = sum(f64(gate)[d, :1] * h[:, unstriped(p)] for d, p in enumerate((pos1, pos2, pos3, pos4)))
    return mxq(f64(w2), 0, "e4m3").T @ mxq(z, 0, "e4m3")

@@ -1,0 +1,244 @@
+from contextlib import ExitStack
+
+import concourse.mybir as mybir
+from concourse.masks import make_identity
+
+K, T, D, V, H, N = 512, 512, 4, 256, 1024, 256
+P = 128
+FLOPS = 2 * K * H * T + 2 * H * N * V
+
+F32 = mybir.dt.float32
+BF16 = mybir.dt.bfloat16
+U32 = mybir.dt.uint32
+U16 = mybir.dt.uint16
+U8 = mybir.dt.uint8
+FP8X4 = mybir.dt.float8_e4m3fn_x4
+MULT = mybir.AluOpType.mult
+RELU = mybir.ActivationFunctionType.Relu
+
+W1_CHUNKS = (128, 128, 256, 256, 256)
+X_CHUNKS = ((0, 256), (256, 128), (384, 128))
+
+
+def tile_picked_gcn_mlp_relu_sub_l_kernel(
+    tc, xT, w1, w2, gate, pos1, pos2, pos3, pos4, out
+):
+    nc = tc.nc
+    with ExitStack() as ctx:
+        keep = ctx.enter_context(tc.tile_pool(name="keep", bufs=1))
+        hpool = ctx.enter_context(tc.tile_pool(name="hpool", bufs=4))
+        gpool = ctx.enter_context(tc.tile_pool(name="gpool", bufs=6))
+        pacc = ctx.enter_context(tc.psum_pool(name="pacc", bufs=2))
+        pone = ctx.enter_context(tc.psum_pool(name="pone", bufs=1))
+
+        def load(name, src, width, queue):
+            raw = keep.tile([P, 4, width], F32, name=name)
+            queue.dma_start(out=raw[:], in_=src.rearrange("(p j) w -> p j w", j=4))
+            return raw
+
+        w1_raw = [load("w1_raw0", w1[:, 0:128], 128, nc.sync)]
+        x_raw = [
+            load("x_raw%d" % i, xT[:, a : a + w], w, nc.sync) for i, (a, w) in enumerate(X_CHUNKS)
+        ]
+        lists = []
+        gates = keep.tile([P, D, V], F32, name="gates")
+        for d, pos in enumerate((pos1, pos2, pos3, pos4)):
+            lst = keep.tile([P, V // 16], U16, name="list%d" % d)
+            nc.sync.dma_start(lst[:], pos)
+            lists.append(lst)
+            if d == 0:
+                nc.sync.dma_start(out=gates[:, 0, :], in_=gate[0])
+        nc.sync.dma_start(out=gates[:, 1:4, :], in_=gate[1:4].rearrange("d p v -> p d v"))
+        c0 = 128
+        for i, width in enumerate(W1_CHUNKS[1:]):
+            w1_raw.append(load("w1_raw%d" % (i + 1), w1[:, c0 : c0 + width], width, nc.sync))
+            c0 += width
+        w2_raw = []
+        for c in range(2):
+            w2_raw.append(load("w2_raw%d" % c, w2[512 * c : 512 * (c + 1), :], N, nc.sync))
+
+        ident = keep.tile([P, P], F32, name="ident")
+        make_identity(nc, ident[:])
+
+        def copy_columns(copy, grouped, raw, a, b):
+            copy(out=grouped[:, a:b, :], in_=raw[:, :, a:b].rearrange("p j w -> p w j"))
+
+        def quantise(name, grouped, width):
+            codes = keep.tile([P, width], U32, align_bytes=64, name=name + "_codes")
+            scales = keep.tile([P, width], U8, align_bytes=64, name=name + "_scales")
+            nc.vector.quantize_mx(
+                out=codes[:].bitcast(FP8X4), scales=scales[:], in_=grouped[:].rearrange("p w j -> p (w j)")
+            )
+            return codes, scales
+
+        w1_g = [
+            keep.tile([P, w, 4], BF16, align_bytes=64, name="w1_g%d" % i) for i, w in enumerate(W1_CHUNKS)
+        ]
+        w2_g = [keep.tile([P, N, 4], BF16, align_bytes=64, name="w2_g%d" % c) for c in range(2)]
+        x_q = []
+        w1_q = []
+
+        def copy_w1(i, half):
+            copy_columns(nc.scalar.copy, w1_g[i], w1_raw[i], 128 * half, 128 * (half + 1))
+
+        def quant_w1(i):
+            codes, scales = quantise("w1_q%d" % i, w1_g[i], W1_CHUNKS[i])
+            for a in range(0, W1_CHUNKS[i], 128):
+                w1_q.append((codes, scales, a))
+
+        def prep_x(i):
+            w = X_CHUNKS[i][1]
+            g = keep.tile([P, w, 4], BF16, align_bytes=64, name="x_g%d" % i)
+            copy_columns(nc.vector.tensor_copy, g, x_raw[i], 0, w)
+            x_q.append(quantise("x_q%d" % i, g, w))
+
+        h_tiles = {}
+
+        def first_product(b):
+            codes, scales, a = w1_q[b]
+            acc = pacc.tile([P, T], F32, name="acc")
+            h = hpool.tile([P, T], F32, name="h")
+            for i, (t0, w) in enumerate(X_CHUNKS):
+                cols = slice(t0, t0 + w)
+                nc.tensor.matmul_mx(
+                    out=acc[:, cols],
+                    lhsT=codes[:, a : a + 128].bitcast(FP8X4),
+                    lhsT_scale=scales[:, a : a + 128],
+                    rhs=x_q[i][0][:].bitcast(FP8X4),
+                    rhs_scale=x_q[i][1][:],
+                    start=True,
+                    stop=True,
+                )
+                if b == 0:
+                    nc.scalar.activation(out=h[:, cols], in_=acc[:, cols], func=RELU)
+            if b > 0:
+                nc.scalar.activation(out=h[:], in_=acc[:], func=RELU)
+            h_tiles[b] = h
+
+        zt_sb = [[None, None], [None, None]]
+        for c in range(2):
+            for vb in range(2):
+                zt_sb[c][vb] = keep.tile([P, 512], BF16, align_bytes=64, name="zt_sb%d%d" % (c, vb))
+        z_codes = []
+        z_scales = []
+        for c in range(2):
+            z_codes.append(keep.tile([P, V], U32, align_bytes=64, name="z_codes%d" % c))
+            z_scales.append(keep.tile([P, V], U8, align_bytes=64, name="z_scales%d" % c))
+
+        zts = {}
+
+        def gathers(b, ds):
+            h = h_tiles[b]
+            if b not in zts:
+                zts[b] = [pone.tile([P, P], F32, name="zt%d" % vb) for vb in range(2)]
+            for d in ds:
+                g = gpool.tile([P, V], F32, name="g")
+                nc.vector.tensor_tensor(g[:], h[:].indirect(lists[d][:]), gates[:, d, :], MULT)
+                for vb in range(2):
+                    nc.tensor.matmul(
+                        zts[b][vb][:],
+                        lhsT=g[:, 128 * vb : 128 * (vb + 1)],
+                        rhs=ident[:],
+                        start=(d == 0),
+                        stop=(d == D - 1),
+                        is_transpose=True,
+                    )
+
+        def leave_zt(b):
+            c, q = divmod(b, 4)
+            for vb in range(2):
+                copy = nc.vector.tensor_copy if (b == 7 and vb == 1) else nc.scalar.copy
+                copy(out=zt_sb[c][vb][:, 128 * q : 128 * (q + 1)], in_=zts[b][vb][:])
+
+        z_g = {}
+
+        def turn_z(c):
+            for vb in range(2):
+                words = zt_sb[c][vb][:].bitcast(F32)
+                wt = pone.tile([P, 2, P], F32, name="wt%d" % vb)
+                for u in range(2):
+                    nc.tensor.transpose(wt[:, u, :], words[:, u::2], ident[:])
+                zg = keep.tile([P, 4 * P], BF16, align_bytes=64, name="zg%d%d" % (c, vb))
+                copy = nc.vector.tensor_copy if (c == 1 and vb == 1) else nc.scalar.copy
+                copy(
+                    out=zg[:].bitcast(F32).rearrange("p (v u) -> p v u", u=2),
+                    in_=wt[:].rearrange("p u v -> p v u"),
+                )
+                z_g[c, vb] = zg
+
+        def quant_z(c):
+            for vb in range(2):
+                cols = slice(128 * vb, 128 * (vb + 1))
+                nc.vector.quantize_mx(
+                    out=z_codes[c][:, cols].bitcast(FP8X4), scales=z_scales[c][:, cols], in_=z_g[c, vb][:]
+                )
+
+        w2_q = {}
+
+        def copy_w2(c, half):
+            copy_columns(nc.scalar.copy, w2_g[c], w2_raw[c], 128 * half, 128 * (half + 1))
+
+        def quant_w2(c):
+            w2_q[c] = quantise("w2_q%d" % c, w2_g[c], N)
+
+        outs = [pone.tile([P, V], F32, name="out_ps%d" % m) for m in range(2)]
+
+        def second_product(c):
+            for m in range(2):
+                rows = slice(128 * m, 128 * (m + 1))
+                nc.tensor.matmul_mx(
+                    out=outs[m][:],
+                    lhsT=w2_q[c][0][:, rows].bitcast(FP8X4),
+                    lhsT_scale=w2_q[c][1][:, rows],
+                    rhs=z_codes[c][:].bitcast(FP8X4),
+                    rhs_scale=z_scales[c][:],
+                    start=(c == 0),
+                    stop=(c == 1),
+                )
+
+        vector_steps = {
+            0: [(quant_w1, (1,))],
+            1: [(quant_w1, (2,))],
+            3: [(quant_w1, (3,))],
+            5: [(quant_w1, (4,))],
+            6: [(quant_w2, (0,)), (quant_z, (0,))],
+            7: [(quant_w2, (1,))],
+        }
+        scalar_steps = {
+            0: [(copy_w1, (2, 0)), (copy_w1, (2, 1))],
+            1: [(copy_w1, (3, 0))],
+            2: [(copy_w1, (3, 1))],
+            3: [(copy_w1, (4, 0)), (copy_w1, (4, 1))],
+            4: [(copy_w2, (0, 0)), (turn_z, (0,))],
+            5: [(copy_w2, (0, 1)), (copy_w2, (1, 0))],
+            6: [(copy_w2, (1, 1))],
+        }
+        copy_w1(0, 0)
+        quant_w1(0)
+        for i in range(3):
+            prep_x(i)
+        first_product(0)
+        copy_w1(1, 0)
+        for b in range(8):
+            gathers(b, (0, 1))
+            for f, args in vector_steps.get(b, []):
+                f(*args)
+            if b + 1 < 8:
+                first_product(b + 1)
+            if b == 6:
+                second_product(0)
+            for f, args in scalar_steps.get(b, []):
+                f(*args)
+            gathers(b, (2, 3))
+            leave_zt(b)
+        turn_z(1)
+        quant_z(1)
+        second_product(1)
+        for m in range(2):
+            res = keep.tile([P, V], F32, name="res%d" % m)
+            if m == 0:
+                nc.vector.tensor_copy(out=res[:], in_=outs[m][:])
+                nc.sync.dma_start(out=out[0:128, :], in_=res[:])
+            else:
+                nc.scalar.copy(out=res[:], in_=outs[m][:])
+                nc.scalar.dma_start(out=out[128:256, :], in_=res[:])

@@ -26,13 +26,16 @@ def tile_picked_gcn_mlp_relu_sub_l_kernel(
     nc = tc.nc
     with ExitStack() as ctx:
         keep = ctx.enter_context(tc.tile_pool(name="keep", bufs=1))
+        ring = ctx.enter_context(tc.tile_pool(name="ring", bufs=2))
+        raws = ctx.enter_context(tc.tile_pool(name="raws", bufs=3))
         hpool = ctx.enter_context(tc.tile_pool(name="hpool", bufs=4))
-        gpool = ctx.enter_context(tc.tile_pool(name="gpool", bufs=6))
+        gpool = ctx.enter_context(tc.tile_pool(name="gpool", bufs=10))
         pacc = ctx.enter_context(tc.psum_pool(name="pacc", bufs=2))
+        pzt = ctx.enter_context(tc.psum_pool(name="pzt", bufs=2))
         pone = ctx.enter_context(tc.psum_pool(name="pone", bufs=1))
 
-        def load(name, src, width, queue):
-            raw = keep.tile([P, 4, width], F32, name=name)
+        def load(name, src, width, queue, pool=keep):
+            raw = pool.tile([P, 4, width], F32, name=name)
             queue.dma_start(out=raw[:], in_=src.rearrange("(p j) w -> p j w", j=4))
             return raw
 
@@ -40,22 +43,22 @@ def tile_picked_gcn_mlp_relu_sub_l_kernel(
         x_raw = [
             load("x_raw%d" % i, xT[:, a : a + w], w, nc.sync) for i, (a, w) in enumerate(X_CHUNKS)
         ]
-        lists = []
+        lists = [keep.tile([P, V // 16], U16, name="list%d" % d) for d in range(D)]
         gates = keep.tile([P, D, V], F32, name="gates")
-        for d, pos in enumerate((pos1, pos2, pos3, pos4)):
-            lst = keep.tile([P, V // 16], U16, name="list%d" % d)
-            nc.sync.dma_start(lst[:], pos)
-            lists.append(lst)
-            if d == 0:
-                nc.sync.dma_start(out=gates[:, 0, :], in_=gate[0])
-        nc.sync.dma_start(out=gates[:, 1:4, :], in_=gate[1:4].rearrange("d p v -> p d v"))
-        c0 = 128
-        for i, width in enumerate(W1_CHUNKS[1:]):
-            w1_raw.append(load("w1_raw%d" % (i + 1), w1[:, c0 : c0 + width], width, nc.sync))
+        w1_raw.append(load("w1_raw1", w1[:, 128:256], 128, nc.sync))
+        nc.sync.dma_start(lists[0][:], pos1)
+        nc.sync.dma_start(out=gates[:], in_=gate.rearrange("d p v -> p d v"))
+        nc.sync.dma_start(lists[1][:], pos2)
+        nc.sync.dma_start(lists[2][:], pos3)
+        nc.sync.dma_start(lists[3][:], pos4)
+        c0 = 256
+        for i, width in enumerate(W1_CHUNKS[2:]):
+            w1_raw.append(load("w_raw", w1[:, c0 : c0 + width], width, nc.sync, raws))
             c0 += width
         w2_raw = []
-        for c in range(2):
-            w2_raw.append(load("w2_raw%d" % c, w2[512 * c : 512 * (c + 1), :], N, nc.sync))
+
+        def load_w2(c):
+            w2_raw.append(load("w_raw", w2[512 * c : 512 * (c + 1), :], N, nc.sync, raws))
 
         ident = keep.tile([P, P], F32, name="ident")
         make_identity(nc, ident[:])
@@ -71,100 +74,115 @@ def tile_picked_gcn_mlp_relu_sub_l_kernel(
             )
             return codes, scales
 
-        w1_g = [
-            keep.tile([P, w, 4], BF16, align_bytes=64, name="w1_g%d" % i) for i, w in enumerate(W1_CHUNKS)
-        ]
-        w2_g = [keep.tile([P, N, 4], BF16, align_bytes=64, name="w2_g%d" % c) for c in range(2)]
+        w1_g = {}
+        w2_g = {}
         x_q = []
         w1_q = []
 
-        def copy_w1(i, half):
-            copy_columns(nc.scalar.copy, w1_g[i], w1_raw[i], 128 * half, 128 * (half + 1))
+        def copy_w1(i, copy=nc.scalar.copy):
+            w = W1_CHUNKS[i]
+            if i < 2:
+                w1_g[i] = keep.tile([P, w, 4], BF16, align_bytes=64, name="w1_g%d" % i)
+            else:
+                w1_g[i] = ring.tile([P, w, 4], BF16, align_bytes=64, name="w_g")
+            copy_columns(copy, w1_g[i], w1_raw[i], 0, w)
 
         def quant_w1(i):
             codes, scales = quantise("w1_q%d" % i, w1_g[i], W1_CHUNKS[i])
             for a in range(0, W1_CHUNKS[i], 128):
                 w1_q.append((codes, scales, a))
 
-        def prep_x(i):
-            w = X_CHUNKS[i][1]
-            g = keep.tile([P, w, 4], BF16, align_bytes=64, name="x_g%d" % i)
-            copy_columns(nc.vector.tensor_copy, g, x_raw[i], 0, w)
-            x_q.append(quantise("x_q%d" % i, g, w))
+        x_g = [
+            keep.tile([P, w, 4], BF16, align_bytes=64, name="x_g%d" % i) for i, (t0, w) in enumerate(X_CHUNKS)
+        ]
+
+        def copy_x(i):
+            copy_columns(nc.vector.tensor_copy, x_g[i], x_raw[i], 0, X_CHUNKS[i][1])
+
+        def quant_x(i):
+            x_q.append(quantise("x_q%d" % i, x_g[i], X_CHUNKS[i][1]))
 
         h_tiles = {}
 
-        def first_product(b):
+        def product_part(b, i, dst):
             codes, scales, a = w1_q[b]
+            nc.tensor.matmul_mx(
+                out=dst,
+                lhsT=codes[:, a : a + 128].bitcast(FP8X4),
+                lhsT_scale=scales[:, a : a + 128],
+                rhs=x_q[i][0][:].bitcast(FP8X4),
+                rhs_scale=x_q[i][1][:],
+                start=True,
+                stop=True,
+            )
+
+        def first_block():
+            h = hpool.tile([P, T], F32, name="h")
+            for i, (t0, w) in enumerate(X_CHUNKS):
+                part = pone.tile([P, w], F32, name=("out_ps0", "wt0", "wt1")[i])
+                product_part(0, i, part[:])
+                if i == 2:
+                    nc.vector.tensor_scalar_max(h[:, t0 : t0 + w], part[:], 0.0)
+                else:
+                    nc.scalar.activation(out=h[:, t0 : t0 + w], in_=part[:], func=RELU)
+            h_tiles[0] = h
+
+        def first_product(b):
             acc = pacc.tile([P, T], F32, name="acc")
             h = hpool.tile([P, T], F32, name="h")
             for i, (t0, w) in enumerate(X_CHUNKS):
-                cols = slice(t0, t0 + w)
-                nc.tensor.matmul_mx(
-                    out=acc[:, cols],
-                    lhsT=codes[:, a : a + 128].bitcast(FP8X4),
-                    lhsT_scale=scales[:, a : a + 128],
-                    rhs=x_q[i][0][:].bitcast(FP8X4),
-                    rhs_scale=x_q[i][1][:],
-                    start=True,
-                    stop=True,
-                )
-                if b == 0:
-                    nc.scalar.activation(out=h[:, cols], in_=acc[:, cols], func=RELU)
-            if b > 0:
-                nc.scalar.activation(out=h[:], in_=acc[:], func=RELU)
+                product_part(b, i, acc[:, t0 : t0 + w])
+            nc.scalar.activation(out=h[:], in_=acc[:], func=RELU)
             h_tiles[b] = h
 
-        zt_sb = [[None, None], [None, None]]
-        for c in range(2):
-            for vb in range(2):
-                zt_sb[c][vb] = keep.tile([P, 512], BF16, align_bytes=64, name="zt_sb%d%d" % (c, vb))
+        zt_sb = [keep.tile([P, 2, 512], BF16, align_bytes=64, name="zt_sb%d" % c) for c in range(2)]
         z_codes = []
         z_scales = []
         for c in range(2):
             z_codes.append(keep.tile([P, V], U32, align_bytes=64, name="z_codes%d" % c))
             z_scales.append(keep.tile([P, V], U8, align_bytes=64, name="z_scales%d" % c))
 
-        zts = {}
+        def gather(b, d, v0=0, v1=V):
+            g = gpool.tile([P, V], F32, name="g")
+            nc.vector.tensor_tensor(
+                g[:, v0:v1],
+                h_tiles[b][:].indirect(lists[d][:, v0 // 16 : v1 // 16]),
+                gates[:, d, v0:v1],
+                MULT,
+            )
+            return g
 
-        def gathers(b, ds):
-            h = h_tiles[b]
-            if b not in zts:
-                zts[b] = [pone.tile([P, P], F32, name="zt%d" % vb) for vb in range(2)]
-            for d in ds:
-                g = gpool.tile([P, V], F32, name="g")
-                nc.vector.tensor_tensor(g[:], h[:].indirect(lists[d][:]), gates[:, d, :], MULT)
-                for vb in range(2):
-                    nc.tensor.matmul(
-                        zts[b][vb][:],
-                        lhsT=g[:, 128 * vb : 128 * (vb + 1)],
-                        rhs=ident[:],
-                        start=(d == 0),
-                        stop=(d == D - 1),
-                        is_transpose=True,
-                    )
+        def add_turned(dst, g, vb, d):
+            nc.tensor.matmul(
+                dst,
+                lhsT=g[:, 128 * vb : 128 * (vb + 1)],
+                rhs=ident[:],
+                start=(d == 0),
+                stop=(d == D - 1),
+                is_transpose=True,
+            )
 
-        def leave_zt(b):
-            c, q = divmod(b, 4)
+        def sum_block(b, gs):
+            zt = pzt.tile([P, 2, P], F32, name="zt")
             for vb in range(2):
-                copy = nc.vector.tensor_copy if (b == 7 and vb == 1) else nc.scalar.copy
-                copy(out=zt_sb[c][vb][:, 128 * q : 128 * (q + 1)], in_=zts[b][vb][:])
+                for d in range(D):
+                    add_turned(zt[:, vb, :], gs[d], vb, d)
+            c, q = divmod(b, 4)
+            nc.scalar.copy(out=zt_sb[c][:, :, 128 * q : 128 * (q + 1)], in_=zt[:])
 
         z_g = {}
 
-        def turn_z(c):
-            for vb in range(2):
-                words = zt_sb[c][vb][:].bitcast(F32)
-                wt = pone.tile([P, 2, P], F32, name="wt%d" % vb)
-                for u in range(2):
-                    nc.tensor.transpose(wt[:, u, :], words[:, u::2], ident[:])
-                zg = keep.tile([P, 4 * P], BF16, align_bytes=64, name="zg%d%d" % (c, vb))
-                copy = nc.vector.tensor_copy if (c == 1 and vb == 1) else nc.scalar.copy
-                copy(
-                    out=zg[:].bitcast(F32).rearrange("p (v u) -> p v u", u=2),
-                    in_=wt[:].rearrange("p u v -> p v u"),
-                )
-                z_g[c, vb] = zg
+        def turn_z(c, vb, copy=nc.scalar.copy):
+            words = zt_sb[c][:, vb, :].bitcast(F32)
+            wt = pone.tile([P, 2, P], F32, name="wt%d" % vb)
+            for u in range(2):
+                nc.tensor.transpose(wt[:, u, :], words[:, u::2], ident[:])
+            zg = keep.tile([P, 4 * P], BF16, align_bytes=64, name="zg%d%d" % (c, vb))
+            copy(
+                out=zg[:].bitcast(F32).rearrange("p (v u) -> p v u", u=2),
+                in_=wt[:].rearrange("p u v -> p v u"),
+            )
+            z_g[c, vb] = zg
 
         def quant_z(c):
             for vb in range(2):
@@ -175,16 +193,19 @@ def tile_picked_gcn_mlp_relu_sub_l_kernel(
 
         w2_q = {}
 
-        def copy_w2(c, half):
-            copy_columns(nc.scalar.copy, w2_g[c], w2_raw[c], 128 * half, 128 * (half + 1))
+        def copy_w2(c):
+            w2_g[c] = ring.tile([P, N, 4], BF16, align_bytes=64, name="w_g")
+            copy_columns(nc.scalar.copy, w2_g[c], w2_raw[c], 0, N)
 
         def quant_w2(c):
             w2_q[c] = quantise("w2_q%d" % c, w2_g[c], N)
 
-        outs = [pone.tile([P, V], F32, name="out_ps%d" % m) for m in range(2)]
+        outs = []
 
         def second_product(c):
             for m in range(2):
+                if c == 0:
+                    outs.append(pone.tile([P, V], F32, name="out_ps%d" % m))
                 rows = slice(128 * m, 128 * (m + 1))
                 nc.tensor.matmul_mx(
                     out=outs[m][:],
@@ -196,42 +217,53 @@ def tile_picked_gcn_mlp_relu_sub_l_kernel(
                     stop=(c == 1),
                 )
 
-        vector_steps = {
-            0: [(quant_w1, (1,))],
-            1: [(quant_w1, (2,))],
-            3: [(quant_w1, (3,))],
-            5: [(quant_w1, (4,))],
-            6: [(quant_w2, (0,)), (quant_z, (0,))],
-            7: [(quant_w2, (1,))],
+        steps = {
+            (1, 0): [(quant_w1, 2), (first_product, 2), (first_product, 3), (copy_w1, 3), (load_w2, 0)],
+            (2, 2): [(quant_w1, 3), (first_product, 4), (first_product, 5)],
+            (3, 0): [(copy_w1, 4), (load_w2, 1)],
+            (4, 1): [(quant_w1, 4), (first_product, 6), (first_product, 7)],
+            (4, 2): [(turn_z, 0, 0), (turn_z, 0, 1), (copy_w2, 0)],
+            (5, 1): [(copy_w2, 1)],
+            (5, 2): [(quant_w2, 0)],
+            (6, 0): [(quant_z, 0)],
+            (6, 1): [(second_product, 0)],
+            (6, 3): [(quant_w2, 1)],
         }
-        scalar_steps = {
-            0: [(copy_w1, (2, 0)), (copy_w1, (2, 1))],
-            1: [(copy_w1, (3, 0))],
-            2: [(copy_w1, (3, 1))],
-            3: [(copy_w1, (4, 0)), (copy_w1, (4, 1))],
-            4: [(copy_w2, (0, 0)), (turn_z, (0,))],
-            5: [(copy_w2, (0, 1)), (copy_w2, (1, 0))],
-            6: [(copy_w2, (1, 1))],
-        }
-        copy_w1(0, 0)
+        copy_w1(0)
+        copy_x(0)
         quant_w1(0)
-        for i in range(3):
-            prep_x(i)
-        first_product(0)
-        copy_w1(1, 0)
-        for b in range(8):
-            gathers(b, (0, 1))
-            for f, args in vector_steps.get(b, []):
-                f(*args)
-            if b + 1 < 8:
-                first_product(b + 1)
-            if b == 6:
-                second_product(0)
-            for f, args in scalar_steps.get(b, []):
-                f(*args)
-            gathers(b, (2, 3))
-            leave_zt(b)
-        turn_z(1)
+        quant_x(0)
+        copy_x(1)
+        copy_x(2)
+        quant_x(1)
+        quant_x(2)
+        first_block()
+        copy_w1(1, nc.vector.tensor_copy)
+        quant_w1(1)
+        first_product(1)
+        copy_w1(2)
+        for b in range(7):
+            gs = []
+            for d in range(D):
+                gs.append(gather(b, d))
+                for step in steps.get((b, d), []):
+                    step[0](*step[1:])
+            sum_block(b, gs)
+
+        gs = [gather(7, d) for d in range(2)]
+        last = []
+        for vb in range(2):
+            zt = pone.tile([P, P], F32, name="wt%d" % vb)
+            last.append(zt)
+            for d in range(2):
+                add_turned(zt[:], gs[d], vb, d)
+        for vb in range(2):
+            copy = (nc.scalar.copy, nc.vector.tensor_copy)[vb]
+            for d in range(2, D):
+                g = gather(7, d, 128 * vb, 128 * (vb + 1))
+                add_turned(last[vb][:], g, vb, d)
+            copy(out=zt_sb[1][:, vb, 384:512], in_=last[vb][:])
+            turn_z(1, vb, copy)
         quant_z(1)
         second_product(1)
         for m in range(2):

@@ -5,6 +5,10 @@ from concourse.masks import make_identity
 
 K, T, D, V, H, N = 512, 512, 4, 256, 1024, 256
 P = 128
+PACK = 4
+BLOCKS = H // P
+HALVES = H // (P * PACK)
+SIDES = V // P
 FLOPS = 2 * K * H * T + 2 * H * N * V
 
 F32 = mybir.dt.float32
@@ -16,8 +20,9 @@ FP8X4 = mybir.dt.float8_e4m3fn_x4
 MULT = mybir.AluOpType.mult
 RELU = mybir.ActivationFunctionType.Relu
 
-W1_CHUNKS = (128, 128, 256, 256, 256)
-X_CHUNKS = ((0, 256), (256, 128), (384, 128))
+X_PIECES = ((0, 256), (256, 128), (384, 128))
+
+W1_PIECES = ((0, 128), (128, 128), (256, 256), (512, 256), (768, 256))
 
 
 def tile_picked_gcn_mlp_relu_sub_l_kernel(
@@ -26,47 +31,58 @@ def tile_picked_gcn_mlp_relu_sub_l_kernel(
     nc = tc.nc
     with ExitStack() as ctx:
         keep = ctx.enter_context(tc.tile_pool(name="keep", bufs=1))
-        ring = ctx.enter_context(tc.tile_pool(name="ring", bufs=2))
+        weights = ctx.enter_context(tc.tile_pool(name="weights", bufs=2))
         raws = ctx.enter_context(tc.tile_pool(name="raws", bufs=3))
-        hpool = ctx.enter_context(tc.tile_pool(name="hpool", bufs=4))
-        gpool = ctx.enter_context(tc.tile_pool(name="gpool", bufs=10))
-        pacc = ctx.enter_context(tc.psum_pool(name="pacc", bufs=2))
-        pzt = ctx.enter_context(tc.psum_pool(name="pzt", bufs=2))
-        pone = ctx.enter_context(tc.psum_pool(name="pone", bufs=1))
+        h_pool = ctx.enter_context(tc.tile_pool(name="h_pool", bufs=4))
+        gathered = ctx.enter_context(tc.tile_pool(name="gathered", bufs=10))
+        psum_h = ctx.enter_context(tc.psum_pool(name="psum_h", bufs=2))
+        psum_sum = ctx.enter_context(tc.psum_pool(name="psum_sum", bufs=2))
+        psum_one = ctx.enter_context(tc.psum_pool(name="psum_one", bufs=1))
 
-        def load(name, src, width, queue, pool=keep):
-            raw = pool.tile([P, 4, width], F32, name=name)
-            queue.dma_start(out=raw[:], in_=src.rearrange("(p j) w -> p j w", j=4))
+
+        def load(pool, name, rows):
+            raw = pool.tile([P, PACK, rows.shape[1]], F32, name=name)
+            nc.sync.dma_start(out=raw[:], in_=rows.rearrange("(p j) w -> p j w", j=PACK))
             return raw
 
-        w1_raw = [load("w1_raw0", w1[:, 0:128], 128, nc.sync)]
-        x_raw = [
-            load("x_raw%d" % i, xT[:, a : a + w], w, nc.sync) for i, (a, w) in enumerate(X_CHUNKS)
-        ]
+        def load_w1(pool, name, piece):
+            first, count = W1_PIECES[piece]
+            return load(pool, name, w1[:, first : first + count])
+
         lists = [keep.tile([P, V // 16], U16, name="list%d" % d) for d in range(D)]
         gates = keep.tile([P, D, V], F32, name="gates")
-        w1_raw.append(load("w1_raw1", w1[:, 128:256], 128, nc.sync))
+
+        w1_raw = [load_w1(keep, "w1_raw0", 0)]
         nc.sync.dma_start(lists[0][:], pos1)
-        nc.sync.dma_start(out=gates[:], in_=gate.rearrange("d p v -> p d v"))
+        x_raw = [
+            load(keep, "x_raw%d" % i, xT[:, first : first + count]) for i, (first, count) in enumerate(X_PIECES)
+        ]
+        nc.sync.dma_start(out=gates[:, 0, :], in_=gate[0])
+        w1_raw.append(load_w1(keep, "w1_raw1", 1))
         nc.sync.dma_start(lists[1][:], pos2)
+        nc.sync.dma_start(out=gates[:, 1:D, :], in_=gate[1:D].rearrange("d p v -> p d v"))
         nc.sync.dma_start(lists[2][:], pos3)
+        w1_raw.append(load_w1(raws, "w_raw", 2))
         nc.sync.dma_start(lists[3][:], pos4)
-        c0 = 256
-        for i, width in enumerate(W1_CHUNKS[2:]):
-            w1_raw.append(load("w_raw", w1[:, c0 : c0 + width], width, nc.sync, raws))
-            c0 += width
+        w1_raw.append(load_w1(raws, "w_raw", 3))
+        w1_raw.append(load_w1(raws, "w_raw", 4))
         w2_raw = []
 
-        def load_w2(c):
-            w2_raw.append(load("w_raw", w2[512 * c : 512 * (c + 1), :], N, nc.sync, raws))
+        def load_w2(half):
+            w2_raw.append(load(raws, "w_raw", w2[512 * half : 512 * (half + 1), :]))
 
-        ident = keep.tile([P, P], F32, name="ident")
-        make_identity(nc, ident[:])
+        identity = keep.tile([P, P], F32, name="identity")
+        make_identity(nc, identity[:])
 
-        def copy_columns(copy, grouped, raw, a, b):
-            copy(out=grouped[:, a:b, :], in_=raw[:, :, a:b].rearrange("p j w -> p w j"))
 
-        def quantise(name, grouped, width):
+        def interleave(copy, grouped, raw):
+            copy(
+                out=grouped[:].rearrange("p (c i) j -> p c j i", i=4),
+                in_=raw[:].rearrange("p j (c i) -> p c j i", i=4),
+            )
+
+        def quantise(name, grouped):
+            width = grouped.shape[1]
             codes = keep.tile([P, width], U32, align_bytes=64, name=name + "_codes")
             scales = keep.tile([P, width], U8, align_bytes=64, name=name + "_scales")
             nc.vector.quantize_mx(
@@ -74,203 +90,220 @@ def tile_picked_gcn_mlp_relu_sub_l_kernel(
             )
             return codes, scales
 
-        w1_g = {}
-        w2_g = {}
-        x_q = []
-        w1_q = []
-
-        def copy_w1(i, copy=nc.scalar.copy):
-            w = W1_CHUNKS[i]
-            if i < 2:
-                w1_g[i] = keep.tile([P, w, 4], BF16, align_bytes=64, name="w1_g%d" % i)
-            else:
-                w1_g[i] = ring.tile([P, w, 4], BF16, align_bytes=64, name="w_g")
-            copy_columns(copy, w1_g[i], w1_raw[i], 0, w)
-
-        def quant_w1(i):
-            codes, scales = quantise("w1_q%d" % i, w1_g[i], W1_CHUNKS[i])
-            for a in range(0, W1_CHUNKS[i], 128):
-                w1_q.append((codes, scales, a))
-
-        x_g = [
-            keep.tile([P, w, 4], BF16, align_bytes=64, name="x_g%d" % i) for i, (t0, w) in enumerate(X_CHUNKS)
+        x_grouped = [
+            keep.tile([P, count, PACK], BF16, align_bytes=64, name="x_grouped%d" % i)
+            for i, (first, count) in enumerate(X_PIECES)
         ]
+        x_quantised = []
 
-        def copy_x(i):
-            copy_columns(nc.vector.tensor_copy, x_g[i], x_raw[i], 0, X_CHUNKS[i][1])
+        def copy_x(piece):
+            interleave(nc.vector.tensor_copy, x_grouped[piece], x_raw[piece])
 
-        def quant_x(i):
-            x_q.append(quantise("x_q%d" % i, x_g[i], X_CHUNKS[i][1]))
+        def quantise_x(piece):
+            x_quantised.append(quantise("x%d" % piece, x_grouped[piece]))
 
-        h_tiles = {}
+        w1_grouped = []
+        w1_quantised = []
 
-        def product_part(b, i, dst):
-            codes, scales, a = w1_q[b]
+        def copy_w1(piece, copy):
+            count = W1_PIECES[piece][1]
+            if count == P:
+                grouped = keep.tile([P, count, PACK], BF16, align_bytes=64, name="w1_grouped%d" % piece)
+            else:
+                grouped = weights.tile([P, count, PACK], BF16, align_bytes=64, name="w_grouped")
+            interleave(copy, grouped, w1_raw[piece])
+            w1_grouped.append(grouped)
+
+        def quantise_w1(piece):
+            codes, scales = quantise("w1_%d" % piece, w1_grouped[piece])
+            for column in range(0, W1_PIECES[piece][1], P):
+                w1_quantised.append((codes, scales, column))
+
+        w2_grouped = []
+        w2_quantised = []
+
+        def copy_w2(half):
+            grouped = weights.tile([P, N, PACK], BF16, align_bytes=64, name="w_grouped")
+            interleave(nc.scalar.copy, grouped, w2_raw[half])
+            w2_grouped.append(grouped)
+
+        def quantise_w2(half):
+            w2_quantised.append(quantise("w2_%d" % half, w2_grouped[half]))
+
+
+        h_tiles = []
+
+        def project(block, piece, result):
+            codes, scales, column = w1_quantised[block]
             nc.tensor.matmul_mx(
-                out=dst,
-                lhsT=codes[:, a : a + 128].bitcast(FP8X4),
-                lhsT_scale=scales[:, a : a + 128],
-                rhs=x_q[i][0][:].bitcast(FP8X4),
-                rhs_scale=x_q[i][1][:],
+                out=result,
+                lhsT=codes[:, column : column + P].bitcast(FP8X4),
+                lhsT_scale=scales[:, column : column + P],
+                rhs=x_quantised[piece][0][:].bitcast(FP8X4),
+                rhs_scale=x_quantised[piece][1][:],
                 start=True,
                 stop=True,
             )
 
-        def first_block():
-            h = hpool.tile([P, T], F32, name="h")
-            for i, (t0, w) in enumerate(X_CHUNKS):
-                part = pone.tile([P, w], F32, name=("out_ps0", "wt0", "wt1")[i])
-                product_part(0, i, part[:])
-                if i == 2:
-                    nc.vector.tensor_scalar_max(h[:, t0 : t0 + w], part[:], 0.0)
+        def first_product_of_block_0():
+            h = h_pool.tile([P, T], F32, name="h")
+            for piece, bank in enumerate(("out0", "turned0", "turned1")):
+                first, count = X_PIECES[piece]
+                result = psum_one.tile([P, count], F32, name=bank)
+                project(0, piece, result[:])
+                if piece == len(X_PIECES) - 1:
+                    nc.vector.tensor_scalar_max(h[:, first : first + count], result[:], 0.0)
                 else:
-                    nc.scalar.activation(out=h[:, t0 : t0 + w], in_=part[:], func=RELU)
-            h_tiles[0] = h
+                    nc.scalar.activation(out=h[:, first : first + count], in_=result[:], func=RELU)
+            h_tiles.append(h)
 
-        def first_product(b):
-            acc = pacc.tile([P, T], F32, name="acc")
-            h = hpool.tile([P, T], F32, name="h")
-            for i, (t0, w) in enumerate(X_CHUNKS):
-                product_part(b, i, acc[:, t0 : t0 + w])
-            nc.scalar.activation(out=h[:], in_=acc[:], func=RELU)
-            h_tiles[b] = h
+        def first_product(block):
+            result = psum_h.tile([P, T], F32, name="result")
+            h = h_pool.tile([P, T], F32, name="h")
+            for piece, (first, count) in enumerate(X_PIECES):
+                project(block, piece, result[:, first : first + count])
+            nc.scalar.activation(out=h[:], in_=result[:], func=RELU)
+            h_tiles.append(h)
 
-        zt_sb = [keep.tile([P, 2, 512], BF16, align_bytes=64, name="zt_sb%d" % c) for c in range(2)]
-        z_codes = []
-        z_scales = []
-        for c in range(2):
-            z_codes.append(keep.tile([P, V], U32, align_bytes=64, name="z_codes%d" % c))
-            z_scales.append(keep.tile([P, V], U8, align_bytes=64, name="z_scales%d" % c))
 
-        def gather(b, d, v0=0, v1=V):
-            g = gpool.tile([P, V], F32, name="g")
+        summed = [
+            keep.tile([P, SIDES, P * PACK], BF16, align_bytes=64, name="summed%d" % half) for half in range(HALVES)
+        ]
+
+        def gather(block, d, first=0, last=V):
+            g = gathered.tile([P, V], F32, name="g")
             nc.vector.tensor_tensor(
-                g[:, v0:v1],
-                h_tiles[b][:].indirect(lists[d][:, v0 // 16 : v1 // 16]),
-                gates[:, d, v0:v1],
+                g[:, first:last],
+                h_tiles[block][:].indirect(lists[d][:, first // 16 : last // 16]),
+                gates[:, d, first:last],
                 MULT,
             )
             return g
 
-        def add_turned(dst, g, vb, d):
+        def add_turned(total, g, side, d):
             nc.tensor.matmul(
-                dst,
-                lhsT=g[:, 128 * vb : 128 * (vb + 1)],
-                rhs=ident[:],
+                total,
+                lhsT=g[:, P * side : P * (side + 1)],
+                rhs=identity[:],
                 start=(d == 0),
                 stop=(d == D - 1),
                 is_transpose=True,
             )
 
-        def sum_block(b, gs):
-            zt = pzt.tile([P, 2, P], F32, name="zt")
-            for vb in range(2):
+        def sum_block(block, gs):
+            total = psum_sum.tile([P, SIDES, P], F32, name="total")
+            for side in range(SIDES):
                 for d in range(D):
-                    add_turned(zt[:, vb, :], gs[d], vb, d)
-            c, q = divmod(b, 4)
-            nc.scalar.copy(out=zt_sb[c][:, :, 128 * q : 128 * (q + 1)], in_=zt[:])
+                    add_turned(total[:, side, :], gs[d], side, d)
+            half, quarter = divmod(block, PACK)
+            nc.scalar.copy(out=summed[half][:, :, P * quarter : P * (quarter + 1)], in_=total[:])
 
-        z_g = {}
 
-        def turn_z(c, vb, copy=nc.scalar.copy):
-            words = zt_sb[c][:, vb, :].bitcast(F32)
-            wt = pone.tile([P, 2, P], F32, name="wt%d" % vb)
+        z_grouped = [
+            keep.tile([P, SIDES, P * PACK], BF16, align_bytes=64, name="z_grouped%d" % half)
+            for half in range(HALVES)
+        ]
+        z_codes = [keep.tile([P, V], U32, align_bytes=64, name="z_codes%d" % half) for half in range(HALVES)]
+        z_scales = [keep.tile([P, V], U8, align_bytes=64, name="z_scales%d" % half) for half in range(HALVES)]
+
+        def turn_back(half, side, copy):
+            words = summed[half][:, side, :].bitcast(F32)
+            turned = psum_one.tile([P, 2, P], F32, name="turned%d" % side)
             for u in range(2):
-                nc.tensor.transpose(wt[:, u, :], words[:, u::2], ident[:])
-            zg = keep.tile([P, 4 * P], BF16, align_bytes=64, name="zg%d%d" % (c, vb))
+                nc.tensor.transpose(turned[:, u, :], words[:, u::2], identity[:])
             copy(
-                out=zg[:].bitcast(F32).rearrange("p (v u) -> p v u", u=2),
-                in_=wt[:].rearrange("p u v -> p v u"),
+                out=z_grouped[half][:, side, :].bitcast(F32).rearrange("p (v u) -> p v u", u=2),
+                in_=turned[:].rearrange("p u v -> p v u"),
             )
-            z_g[c, vb] = zg
 
-        def quant_z(c):
-            for vb in range(2):
-                cols = slice(128 * vb, 128 * (vb + 1))
-                nc.vector.quantize_mx(
-                    out=z_codes[c][:, cols].bitcast(FP8X4), scales=z_scales[c][:, cols], in_=z_g[c, vb][:]
-                )
+        def quantise_z(half, first_side, last_side):
+            columns = slice(P * first_side, P * last_side)
+            nc.vector.quantize_mx(
+                out=z_codes[half][:, columns].bitcast(FP8X4),
+                scales=z_scales[half][:, columns],
+                in_=z_grouped[half][:, first_side:last_side, :].rearrange("p s w -> p (s w)"),
+            )
 
-        w2_q = {}
+        out_banks = []
 
-        def copy_w2(c):
-            w2_g[c] = ring.tile([P, N, 4], BF16, align_bytes=64, name="w_g")
-            copy_columns(nc.scalar.copy, w2_g[c], w2_raw[c], 0, N)
-
-        def quant_w2(c):
-            w2_q[c] = quantise("w2_q%d" % c, w2_g[c], N)
-
-        outs = []
-
-        def second_product(c):
-            for m in range(2):
-                if c == 0:
-                    outs.append(pone.tile([P, V], F32, name="out_ps%d" % m))
-                rows = slice(128 * m, 128 * (m + 1))
+        def second_product(half):
+            for rows in range(N // P):
+                if half == 0:
+                    out_banks.append(psum_one.tile([P, V], F32, name="out%d" % rows))
+                columns = slice(P * rows, P * (rows + 1))
                 nc.tensor.matmul_mx(
-                    out=outs[m][:],
-                    lhsT=w2_q[c][0][:, rows].bitcast(FP8X4),
-                    lhsT_scale=w2_q[c][1][:, rows],
-                    rhs=z_codes[c][:].bitcast(FP8X4),
-                    rhs_scale=z_scales[c][:],
-                    start=(c == 0),
-                    stop=(c == 1),
+                    out=out_banks[rows][:],
+                    lhsT=w2_quantised[half][0][:, columns].bitcast(FP8X4),
+                    lhsT_scale=w2_quantised[half][1][:, columns],
+                    rhs=z_codes[half][:].bitcast(FP8X4),
+                    rhs_scale=z_scales[half][:],
+                    start=(half == 0),
+                    stop=(half == HALVES - 1),
                 )
 
+
+        scalar_copy = nc.scalar.copy
         steps = {
-            (1, 0): [(quant_w1, 2), (first_product, 2), (first_product, 3), (copy_w1, 3), (load_w2, 0)],
-            (2, 2): [(quant_w1, 3), (first_product, 4), (first_product, 5)],
-            (3, 0): [(copy_w1, 4), (load_w2, 1)],
-            (4, 1): [(quant_w1, 4), (first_product, 6), (first_product, 7)],
-            (4, 2): [(turn_z, 0, 0), (turn_z, 0, 1), (copy_w2, 0)],
+            (1, 0): [
+                (quantise_w1, 2),
+                (first_product, 2),
+                (first_product, 3),
+                (copy_w1, 3, scalar_copy),
+                (load_w2, 0),
+            ],
+            (2, 2): [(quantise_w1, 3), (first_product, 4), (first_product, 5)],
+            (3, 0): [(copy_w1, 4, scalar_copy), (load_w2, 1)],
+            (4, 1): [(quantise_w1, 4), (first_product, 6), (first_product, 7)],
+            (4, 2): [(turn_back, 0, 0, scalar_copy), (turn_back, 0, 1, scalar_copy), (copy_w2, 0)],
             (5, 1): [(copy_w2, 1)],
-            (5, 2): [(quant_w2, 0)],
-            (6, 0): [(quant_z, 0)],
+            (5, 2): [(quantise_w2, 0)],
+            (6, 0): [(quantise_z, 0, 0, SIDES)],
             (6, 1): [(second_product, 0)],
-            (6, 3): [(quant_w2, 1)],
+            (6, 3): [(quantise_w2, 1)],
         }
-        copy_w1(0)
+
+        copy_w1(0, scalar_copy)
         copy_x(0)
-        quant_w1(0)
-        quant_x(0)
+        quantise_w1(0)
+        quantise_x(0)
         copy_x(1)
         copy_x(2)
-        quant_x(1)
-        quant_x(2)
-        first_block()
+        quantise_x(1)
+        quantise_x(2)
+        first_product_of_block_0()
         copy_w1(1, nc.vector.tensor_copy)
-        quant_w1(1)
+        quantise_w1(1)
         first_product(1)
-        copy_w1(2)
-        for b in range(7):
+        copy_w1(2, scalar_copy)
+
+        for block in range(BLOCKS - 1):
             gs = []
             for d in range(D):
-                gs.append(gather(b, d))
-                for step in steps.get((b, d), []):
+                gs.append(gather(block, d))
+                for step in steps.get((block, d), []):
                     step[0](*step[1:])
-            sum_block(b, gs)
+            sum_block(block, gs)
 
-        gs = [gather(7, d) for d in range(2)]
-        last = []
-        for vb in range(2):
-            zt = pone.tile([P, P], F32, name="wt%d" % vb)
-            last.append(zt)
+        last = BLOCKS - 1
+        copies = (nc.scalar.copy, nc.vector.tensor_copy)
+        gs = [gather(last, d) for d in range(2)]
+        totals = []
+        for side in range(SIDES):
+            total = psum_one.tile([P, P], F32, name="turned%d" % side)
+            totals.append(total)
             for d in range(2):
-                add_turned(zt[:], gs[d], vb, d)
-        for vb in range(2):
-            copy = (nc.scalar.copy, nc.vector.tensor_copy)[vb]
+                add_turned(total[:], gs[d], side, d)
+        for side in range(SIDES):
             for d in range(2, D):
-                g = gather(7, d, 128 * vb, 128 * (vb + 1))
-                add_turned(last[vb][:], g, vb, d)
-            copy(out=zt_sb[1][:, vb, 384:512], in_=last[vb][:])
-            turn_z(1, vb, copy)
-        quant_z(1)
+                g = gather(last, d, P * side, P * (side + 1))
+                add_turned(totals[side][:], g, side, d)
+            copies[side](out=summed[1][:, side, P * (PACK - 1) : P * PACK], in_=totals[side][:])
+            turn_back(1, side, copies[side])
+        for side in range(SIDES):
+            quantise_z(1, side, side + 1)
         second_product(1)
-        for m in range(2):
-            res = keep.tile([P, V], F32, name="res%d" % m)
-            if m == 0:
-                nc.vector.tensor_copy(out=res[:], in_=outs[m][:])
-                nc.sync.dma_start(out=out[0:128, :], in_=res[:])
-            else:
-                nc.scalar.copy(out=res[:], in_=outs[m][:])
-                nc.scalar.dma_start(out=out[128:256, :], in_=res[:])
+
+        for rows, (copy, queue) in enumerate(((nc.vector.tensor_copy, nc.sync), (nc.scalar.copy, nc.scalar))):
+            result = keep.tile([P, V], F32, name="stored%d" % rows)
+            copy(out=result[:], in_=out_banks[rows][:])
+            queue.dma_start(out=out[P * rows : P * (rows + 1), :], in_=result[:])

@@ -57,8 +57,8 @@ def tile_picked_gcn_mlp_relu_sub_l_kernel(
         x_raw = [
             load(keep, "x_raw%d" % i, xT[:, first : first + count]) for i, (first, count) in enumerate(X_PIECES)
         ]
-        nc.sync.dma_start(out=gates[:, 0, :], in_=gate[0])
         w1_raw.append(load_w1(keep, "w1_raw1", 1))
+        nc.sync.dma_start(out=gates[:, 0, :], in_=gate[0])
         nc.sync.dma_start(lists[1][:], pos2)
         nc.sync.dma_start(out=gates[:, 1:D, :], in_=gate[1:D].rearrange("d p v -> p d v"))
         nc.sync.dma_start(lists[2][:], pos3)

from contextlib import ExitStack

import concourse.mybir as mybir
from concourse.masks import make_identity

K, T, D, V, H, N = 512, 512, 4, 256, 1024, 256
P = 128
PACK = 4
BLOCKS = H // P
HALVES = H // (P * PACK)
SIDES = V // P
FLOPS = 2 * K * H * T + 2 * H * N * V

F32 = mybir.dt.float32
BF16 = mybir.dt.bfloat16
U32 = mybir.dt.uint32
U16 = mybir.dt.uint16
U8 = mybir.dt.uint8
FP8X4 = mybir.dt.float8_e4m3fn_x4
MULT = mybir.AluOpType.mult
RELU = mybir.ActivationFunctionType.Relu

X_PIECES = ((0, 256), (256, 128), (384, 128))

W1_PIECES = ((0, 128), (128, 128), (256, 256), (512, 256), (768, 256))


def tile_picked_gcn_mlp_relu_sub_l_kernel(
    tc, xT, w1, w2, gate, pos1, pos2, pos3, pos4, out
):
    nc = tc.nc
    with ExitStack() as ctx:
        keep = ctx.enter_context(tc.tile_pool(name="keep", bufs=1))
        weights = ctx.enter_context(tc.tile_pool(name="weights", bufs=2))
        raws = ctx.enter_context(tc.tile_pool(name="raws", bufs=3))
        h_pool = ctx.enter_context(tc.tile_pool(name="h_pool", bufs=4))
        gathered = ctx.enter_context(tc.tile_pool(name="gathered", bufs=10))
        psum_h = ctx.enter_context(tc.psum_pool(name="psum_h", bufs=2))
        psum_sum = ctx.enter_context(tc.psum_pool(name="psum_sum", bufs=2))
        psum_one = ctx.enter_context(tc.psum_pool(name="psum_one", bufs=1))


        def load(pool, name, rows):
            raw = pool.tile([P, PACK, rows.shape[1]], F32, name=name)
            nc.sync.dma_start(out=raw[:], in_=rows.rearrange("(p j) w -> p j w", j=PACK))
            return raw

        def load_w1(pool, name, piece):
            first, count = W1_PIECES[piece]
            return load(pool, name, w1[:, first : first + count])

        lists = [keep.tile([P, V // 16], U16, name="list%d" % d) for d in range(D)]
        gates = keep.tile([P, D, V], F32, name="gates")

        w1_raw = [load_w1(keep, "w1_raw0", 0)]
        nc.sync.dma_start(lists[0][:], pos1)
        x_raw = [
            load(keep, "x_raw%d" % i, xT[:, first : first + count]) for i, (first, count) in enumerate(X_PIECES)
        ]
        w1_raw.append(load_w1(keep, "w1_raw1", 1))
        nc.sync.dma_start(out=gates[:, 0, :], in_=gate[0])
        nc.sync.dma_start(lists[1][:], pos2)
        nc.sync.dma_start(out=gates[:, 1:D, :], in_=gate[1:D].rearrange("d p v -> p d v"))
        nc.sync.dma_start(lists[2][:], pos3)
        w1_raw.append(load_w1(raws, "w_raw", 2))
        nc.sync.dma_start(lists[3][:], pos4)
        w1_raw.append(load_w1(raws, "w_raw", 3))
        w1_raw.append(load_w1(raws, "w_raw", 4))
        w2_raw = []

        def load_w2(half):
            w2_raw.append(load(raws, "w_raw", w2[512 * half : 512 * (half + 1), :]))

        identity = keep.tile([P, P], F32, name="identity")
        make_identity(nc, identity[:])


        def interleave(copy, grouped, raw):
            copy(
                out=grouped[:].rearrange("p (c i) j -> p c j i", i=4),
                in_=raw[:].rearrange("p j (c i) -> p c j i", i=4),
            )

        def quantise(name, grouped):
            width = grouped.shape[1]
            codes = keep.tile([P, width], U32, align_bytes=64, name=name + "_codes")
            scales = keep.tile([P, width], U8, align_bytes=64, name=name + "_scales")
            nc.vector.quantize_mx(
                out=codes[:].bitcast(FP8X4), scales=scales[:], in_=grouped[:].rearrange("p w j -> p (w j)")
            )
            return codes, scales

        x_grouped = [
            keep.tile([P, count, PACK], BF16, align_bytes=64, name="x_grouped%d" % i)
            for i, (first, count) in enumerate(X_PIECES)
        ]
        x_quantised = []

        def copy_x(piece):
            interleave(nc.vector.tensor_copy, x_grouped[piece], x_raw[piece])

        def quantise_x(piece):
            x_quantised.append(quantise("x%d" % piece, x_grouped[piece]))

        w1_grouped = []
        w1_quantised = []

        def copy_w1(piece, copy):
            count = W1_PIECES[piece][1]
            if count == P:
                grouped = keep.tile([P, count, PACK], BF16, align_bytes=64, name="w1_grouped%d" % piece)
            else:
                grouped = weights.tile([P, count, PACK], BF16, align_bytes=64, name="w_grouped")
            interleave(copy, grouped, w1_raw[piece])
            w1_grouped.append(grouped)

        def quantise_w1(piece):
            codes, scales = quantise("w1_%d" % piece, w1_grouped[piece])
            for column in range(0, W1_PIECES[piece][1], P):
                w1_quantised.append((codes, scales, column))

        w2_grouped = []
        w2_quantised = []

        def copy_w2(half):
            grouped = weights.tile([P, N, PACK], BF16, align_bytes=64, name="w_grouped")
            interleave(nc.scalar.copy, grouped, w2_raw[half])
            w2_grouped.append(grouped)

        def quantise_w2(half):
            w2_quantised.append(quantise("w2_%d" % half, w2_grouped[half]))


        h_tiles = []

        def project(block, piece, result):
            codes, scales, column = w1_quantised[block]
            nc.tensor.matmul_mx(
                out=result,
                lhsT=codes[:, column : column + P].bitcast(FP8X4),
                lhsT_scale=scales[:, column : column + P],
                rhs=x_quantised[piece][0][:].bitcast(FP8X4),
                rhs_scale=x_quantised[piece][1][:],
                start=True,
                stop=True,
            )

        def first_product_of_block_0():
            h = h_pool.tile([P, T], F32, name="h")
            for piece, bank in enumerate(("out0", "turned0", "turned1")):
                first, count = X_PIECES[piece]
                result = psum_one.tile([P, count], F32, name=bank)
                project(0, piece, result[:])
                if piece == len(X_PIECES) - 1:
                    nc.vector.tensor_scalar_max(h[:, first : first + count], result[:], 0.0)
                else:
                    nc.scalar.activation(out=h[:, first : first + count], in_=result[:], func=RELU)
            h_tiles.append(h)

        def first_product(block):
            result = psum_h.tile([P, T], F32, name="result")
            h = h_pool.tile([P, T], F32, name="h")
            for piece, (first, count) in enumerate(X_PIECES):
                project(block, piece, result[:, first : first + count])
            nc.scalar.activation(out=h[:], in_=result[:], func=RELU)
            h_tiles.append(h)


        summed = [
            keep.tile([P, SIDES, P * PACK], BF16, align_bytes=64, name="summed%d" % half) for half in range(HALVES)
        ]

        def gather(block, d, first=0, last=V):
            g = gathered.tile([P, V], F32, name="g")
            nc.vector.tensor_tensor(
                g[:, first:last],
                h_tiles[block][:].indirect(lists[d][:, first // 16 : last // 16]),
                gates[:, d, first:last],
                MULT,
            )
            return g

        def add_turned(total, g, side, d):
            nc.tensor.matmul(
                total,
                lhsT=g[:, P * side : P * (side + 1)],
                rhs=identity[:],
                start=(d == 0),
                stop=(d == D - 1),
                is_transpose=True,
            )

        def sum_block(block, gs):
            total = psum_sum.tile([P, SIDES, P], F32, name="total")
            for side in range(SIDES):
                for d in range(D):
                    add_turned(total[:, side, :], gs[d], side, d)
            half, quarter = divmod(block, PACK)
            nc.scalar.copy(out=summed[half][:, :, P * quarter : P * (quarter + 1)], in_=total[:])


        z_grouped = [
            keep.tile([P, SIDES, P * PACK], BF16, align_bytes=64, name="z_grouped%d" % half)
            for half in range(HALVES)
        ]
        z_codes = [keep.tile([P, V], U32, align_bytes=64, name="z_codes%d" % half) for half in range(HALVES)]
        z_scales = [keep.tile([P, V], U8, align_bytes=64, name="z_scales%d" % half) for half in range(HALVES)]

        def turn_back(half, side, copy):
            words = summed[half][:, side, :].bitcast(F32)
            turned = psum_one.tile([P, 2, P], F32, name="turned%d" % side)
            for u in range(2):
                nc.tensor.transpose(turned[:, u, :], words[:, u::2], identity[:])
            copy(
                out=z_grouped[half][:, side, :].bitcast(F32).rearrange("p (v u) -> p v u", u=2),
                in_=turned[:].rearrange("p u v -> p v u"),
            )

        def quantise_z(half, first_side, last_side):
            columns = slice(P * first_side, P * last_side)
            nc.vector.quantize_mx(
                out=z_codes[half][:, columns].bitcast(FP8X4),
                scales=z_scales[half][:, columns],
                in_=z_grouped[half][:, first_side:last_side, :].rearrange("p s w -> p (s w)"),
            )

        out_banks = []

        def second_product(half):
            for rows in range(N // P):
                if half == 0:
                    out_banks.append(psum_one.tile([P, V], F32, name="out%d" % rows))
                columns = slice(P * rows, P * (rows + 1))
                nc.tensor.matmul_mx(
                    out=out_banks[rows][:],
                    lhsT=w2_quantised[half][0][:, columns].bitcast(FP8X4),
                    lhsT_scale=w2_quantised[half][1][:, columns],
                    rhs=z_codes[half][:].bitcast(FP8X4),
                    rhs_scale=z_scales[half][:],
                    start=(half == 0),
                    stop=(half == HALVES - 1),
                )


        scalar_copy = nc.scalar.copy
        steps = {
            (1, 0): [
                (quantise_w1, 2),
                (first_product, 2),
                (first_product, 3),
                (copy_w1, 3, scalar_copy),
                (load_w2, 0),
            ],
            (2, 2): [(quantise_w1, 3), (first_product, 4), (first_product, 5)],
            (3, 0): [(copy_w1, 4, scalar_copy), (load_w2, 1)],
            (4, 1): [(quantise_w1, 4), (first_product, 6), (first_product, 7)],
            (4, 2): [(turn_back, 0, 0, scalar_copy), (turn_back, 0, 1, scalar_copy), (copy_w2, 0)],
            (5, 1): [(copy_w2, 1)],
            (5, 2): [(quantise_w2, 0)],
            (6, 0): [(quantise_z, 0, 0, SIDES)],
            (6, 1): [(second_product, 0)],
            (6, 3): [(quantise_w2, 1)],
        }

        copy_w1(0, scalar_copy)
        copy_x(0)
        quantise_w1(0)
        quantise_x(0)
        copy_x(1)
        copy_x(2)
        quantise_x(1)
        quantise_x(2)
        first_product_of_block_0()
        copy_w1(1, nc.vector.tensor_copy)
        quantise_w1(1)
        first_product(1)
        copy_w1(2, scalar_copy)

        for block in range(BLOCKS - 1):
            gs = []
            for d in range(D):
                gs.append(gather(block, d))
                for step in steps.get((block, d), []):
                    step[0](*step[1:])
            sum_block(block, gs)

        last = BLOCKS - 1
        copies = (nc.scalar.copy, nc.vector.tensor_copy)
        gs = [gather(last, d) for d in range(2)]
        totals = []
        for side in range(SIDES):
            total = psum_one.tile([P, P], F32, name="turned%d" % side)
            totals.append(total)
            for d in range(2):
                add_turned(total[:], gs[d], side, d)
        for side in range(SIDES):
            for d in range(2, D):
                g = gather(last, d, P * side, P * (side + 1))
                add_turned(totals[side][:], g, side, d)
            copies[side](out=summed[1][:, side, P * (PACK - 1) : P * PACK], in_=totals[side][:])
            turn_back(1, side, copies[side])
        for side in range(SIDES):
            quantise_z(1, side, side + 1)
        second_product(1)

        for rows, (copy, queue) in enumerate(((nc.vector.tensor_copy, nc.sync), (nc.scalar.copy, nc.scalar))):
            result = keep.tile([P, V], F32, name="stored%d" % rows)
            copy(out=result[:], in_=out_banks[rows][:])
            queue.dma_start(out=out[P * rows : P * (rows + 1), :], in_=result[:])
